import numpy as np
import ml_dtypes

BF16 = ml_dtypes.bfloat16


def bf(x):
    return np.asarray(x, np.float32).astype(BF16)


def f32(x):
    return np.asarray(x, np.float32)


def f64(x):
    return np.asarray(x).astype(np.float64)


def striped(idx):
    return np.tile(idx.reshape(-1, 16).T, (8, 1))


S, K, M, N, B, Q = 256, 128, 256, 192, 2, 96


def setup_inputs():
    return {"base": bf(np.random.standard_normal((B, M, S))), "x": bf(np.random.standard_normal((K, N))), "w": bf(np.random.standard_normal((K, M)) / np.sqrt(K)), "s": f32(0.5 + np.random.random_sample((M, 1))), "b": f32(0.5 * np.random.standard_normal((M, 1))), "offs": striped(np.random.permutation(S)[:N])}


def reference(base, x, w, s, b, offs):
    idx = offs[:16].T.reshape(-1)
    z = f64(base).copy()
    for i in range(B):
        z[i][:, idx[i * Q : (i + 1) * Q]] = f64(w).T @ f64(x)[:, i * Q : (i + 1) * Q]
    return z * f64(s) + f64(b)

@@ -1,0 +1,73 @@
+import concourse.mybir as mybir
+from concourse.masks import make_identity
+
+BF16, F32, U16 = mybir.dt.bfloat16, mybir.dt.float32, mybir.dt.uint16
+P = 128
+FLOPS = 2 * 128 * 256 * 192 + 2 * 2 * 256 * 256
+
+
+def tile_scatter_matmul_kernel(tc, base, x, w, s, b, offs, out):
+    nc = tc.nc
+    seqs, feats, tokens = base.shape
+    entries = x.shape[1]
+    blocks = feats // P
+    piece = entries // seqs
+    piece_cols = piece // 16
+
+    with (
+        tc.tile_pool(name="held", bufs=1) as held,
+        tc.psum_pool(name="psum", bufs=1) as psum,
+    ):
+        base_t = held.tile([P, seqs * blocks, tokens], BF16)
+        offs_t = held.tile([P, entries // 16], U16)
+        w_t = held.tile([P, feats], BF16)
+        x_t = held.tile([P, entries], BF16)
+        gain = held.tile([P, blocks], F32)
+        shift = held.tile([P, blocks], F32)
+        nc.sync.dma_start(base_t[:], base.rearrange("i (a p) t -> p (i a) t", p=P))
+        nc.sync.dma_start(offs_t[:], offs)
+        nc.sync.dma_start(w_t[:], w)
+        nc.sync.dma_start(x_t[:], x)
+        nc.scalar.dma_start(gain[:], s.rearrange("(a p) o -> p (a o)", p=P))
+        nc.scalar.dma_start(shift[:], b.rearrange("(a p) o -> p (a o)", p=P))
+
+        ident = held.tile([P, P], BF16)
+        make_identity(nc, ident[:])
+
+        windows = [psum.tile([P, tokens], F32, name=f"window{n}") for n in range(seqs * blocks)]
+        for n, window in enumerate(windows):
+            nc.tensor.matmul(window[:], ident[:], base_t[:, n, :], start=True, stop=True)
+
+        for n, window in enumerate(windows):
+            i, a = divmod(n, blocks)
+            places = offs_t[:, i * piece_cols : (i + 1) * piece_cols]
+            nc.tensor.matmul(
+                window[:].indirect(places),
+                w_t[:, a * P : (a + 1) * P],
+                x_t[:, i * piece : (i + 1) * piece],
+                start=True,
+                stop=True,
+            )
+
+        out_rows = out.rearrange("i (a p) t -> p (i a) t", p=P)
+        for n, window in enumerate(windows):
+            a = n % blocks
+            result = held.tile([P, tokens], F32, name=f"result{n}")
+            if n % 2 == 0:
+                nc.vector.tensor_scalar(
+                    result[:],
+                    window[:],
+                    gain[:, a : a + 1],
+                    shift[:, a : a + 1],
+                    op0=mybir.AluOpType.mult,
+                    op1=mybir.AluOpType.add,
+                )
+            else:
+                nc.scalar.activation(
+                    result[:],
+                    window[:],
+                    mybir.ActivationFunctionType.Identity,
+                    bias=shift[:, a : a + 1],
+                    scale=gain[:, a : a + 1],
+                )
+            nc.sync.dma_start(out_rows[:, n, :], result[:])

@@ -18,56 +18,60 @@ def tile_scatter_matmul_kernel(tc, base, x, w, s, b, offs, out):
         tc.tile_pool(name="held", bufs=1) as held,
         tc.psum_pool(name="psum", bufs=1) as psum,
     ):
-        base_t = held.tile([P, seqs * blocks, tokens], BF16)
+        base_t = held.tile([P, seqs, blocks * tokens], BF16)
         offs_t = held.tile([P, entries // 16], U16)
         w_t = held.tile([P, feats], BF16)
         x_t = held.tile([P, entries], BF16)
         gain = held.tile([P, blocks], F32)
         shift = held.tile([P, blocks], F32)
-        nc.sync.dma_start(base_t[:], base.rearrange("i (a p) t -> p (i a) t", p=P))
+        nc.sync.dma_start(base_t[:], base.rearrange("i (p a) t -> p i (a t)", p=P))
         nc.sync.dma_start(offs_t[:], offs)
         nc.sync.dma_start(w_t[:], w)
         nc.sync.dma_start(x_t[:], x)
-        nc.scalar.dma_start(gain[:], s.rearrange("(a p) o -> p (a o)", p=P))
-        nc.scalar.dma_start(shift[:], b.rearrange("(a p) o -> p (a o)", p=P))
+        nc.scalar.dma_start(gain[:], s.rearrange("(p a) o -> p (a o)", p=P))
+        nc.scalar.dma_start(shift[:], b.rearrange("(p a) o -> p (a o)", p=P))
 
         ident = held.tile([P, P], BF16)
         make_identity(nc, ident[:])
 
         windows = [psum.tile([P, tokens], F32, name=f"window{n}") for n in range(seqs * blocks)]
         for n, window in enumerate(windows):
-            nc.tensor.matmul(window[:], ident[:], base_t[:, n, :], start=True, stop=True)
+            i, a = divmod(n, blocks)
+            rows = base_t[:, i, a * tokens : (a + 1) * tokens]
+            nc.tensor.matmul(window[:], ident[:], rows, start=True, stop=True)
 
         for n, window in enumerate(windows):
             i, a = divmod(n, blocks)
             places = offs_t[:, i * piece_cols : (i + 1) * piece_cols]
             nc.tensor.matmul(
                 window[:].indirect(places),
-                w_t[:, a * P : (a + 1) * P],
+                w_t[:, a::blocks],
                 x_t[:, i * piece : (i + 1) * piece],
                 start=True,
                 stop=True,
             )
 
-        out_rows = out.rearrange("i (a p) t -> p (i a) t", p=P)
-        for n, window in enumerate(windows):
-            a = n % blocks
-            result = held.tile([P, tokens], F32, name=f"result{n}")
-            if n % 2 == 0:
-                nc.vector.tensor_scalar(
-                    result[:],
-                    window[:],
-                    gain[:, a : a + 1],
-                    shift[:, a : a + 1],
-                    op0=mybir.AluOpType.mult,
-                    op1=mybir.AluOpType.add,
-                )
-            else:
-                nc.scalar.activation(
-                    result[:],
-                    window[:],
-                    mybir.ActivationFunctionType.Identity,
-                    bias=shift[:, a : a + 1],
-                    scale=gain[:, a : a + 1],
-                )
-            nc.sync.dma_start(out_rows[:, n, :], result[:])
+        out_rows = out.rearrange("i (p a) t -> p i (a t)", p=P)
+        for i in range(seqs):
+            result = held.tile([P, blocks * tokens], F32, name=f"result{i}")
+            for a in range(blocks):
+                window = windows[i * blocks + a]
+                part = result[:, a * tokens : (a + 1) * tokens]
+                if a == 0:
+                    nc.vector.tensor_scalar(
+                        part,
+                        window[:],
+                        gain[:, a : a + 1],
+                        shift[:, a : a + 1],
+                        op0=mybir.AluOpType.mult,
+                        op1=mybir.AluOpType.add,
+                    )
+                else:
+                    nc.scalar.activation(
+                        part,
+                        window[:],
+                        mybir.ActivationFunctionType.Identity,
+                        bias=shift[:, a : a + 1],
+                        scale=gain[:, a : a + 1],
+                    )
+            nc.sync.dma_start(out_rows[:, i, :], result[:])

@@ -28,8 +28,12 @@ def tile_scatter_matmul_kernel(tc, base, x, w, s, b, offs, out):
         nc.sync.dma_start(offs_t[:], offs)
         nc.sync.dma_start(w_t[:], w)
         nc.sync.dma_start(x_t[:], x)
-        nc.scalar.dma_start(gain[:], s.rearrange("(p a) o -> p (a o)", p=P))
-        nc.scalar.dma_start(shift[:], b.rearrange("(p a) o -> p (a o)", p=P))
+        nc.sync.dma_start(gain[:], s.rearrange("(p a) o -> p (a o)", p=P))
+        nc.sync.dma_start(shift[:], b.rearrange("(p a) o -> p (a o)", p=P))
+
+        early = held.tile([P, 1], F32)
+        nc.vector.memset(early[:], 0.0)
+        nc.scalar.activation(early[:], early[:], mybir.ActivationFunctionType.Identity)
 
         ident = held.tile([P, P], BF16)
         make_identity(nc, ident[:])

@@ -24,7 +24,9 @@ def tile_scatter_matmul_kernel(tc, base, x, w, s, b, offs, out):
         x_t = held.tile([P, entries], BF16)
         gain = held.tile([P, blocks], F32)
         shift = held.tile([P, blocks], F32)
-        nc.sync.dma_start(base_t[:], base.rearrange("i (p a) t -> p i (a t)", p=P))
+        base_rows = base.rearrange("i (p a) t -> p i (a t)", p=P)
+        for i in range(seqs):
+            nc.sync.dma_start(base_t[:, i, :], base_rows[:, i, :])
         nc.sync.dma_start(offs_t[:], offs)
         nc.sync.dma_start(w_t[:], w)
         nc.sync.dma_start(x_t[:], x)
@@ -57,13 +59,12 @@ def tile_scatter_matmul_kernel(tc, base, x, w, s, b, offs, out):
 
         out_rows = out.rearrange("i (p a) t -> p i (a t)", p=P)
         for i in range(seqs):
-            result = held.tile([P, blocks * tokens], F32, name=f"result{i}")
             for a in range(blocks):
                 window = windows[i * blocks + a]
-                part = result[:, a * tokens : (a + 1) * tokens]
+                result = held.tile([P, tokens], F32, name=f"result{i}_{a}")
                 if a == 0:
                     nc.vector.tensor_scalar(
-                        part,
+                        result[:],
                         window[:],
                         gain[:, a : a + 1],
                         shift[:, a : a + 1],
@@ -72,10 +73,10 @@ def tile_scatter_matmul_kernel(tc, base, x, w, s, b, offs, out):
                     )
                 else:
                     nc.scalar.activation(
-                        part,
+                        result[:],
                         window[:],
                         mybir.ActivationFunctionType.Identity,
                         bias=shift[:, a : a + 1],
                         scale=gain[:, a : a + 1],
                     )
-            nc.sync.dma_start(out_rows[:, i, :], result[:])
+                nc.sync.dma_start(out_rows[:, i, a * tokens : (a + 1) * tokens], result[:])

import concourse.mybir as mybir
from concourse.masks import make_identity

BF16, F32, U16 = mybir.dt.bfloat16, mybir.dt.float32, mybir.dt.uint16
P = 128
FLOPS = 2 * 128 * 256 * 192 + 2 * 2 * 256 * 256


def tile_scatter_matmul_kernel(tc, base, x, w, s, b, offs, out):
    nc = tc.nc
    seqs, feats, tokens = base.shape
    entries = x.shape[1]
    blocks = feats // P
    piece = entries // seqs
    piece_cols = piece // 16

    with (
        tc.tile_pool(name="held", bufs=1) as held,
        tc.psum_pool(name="psum", bufs=1) as psum,
    ):
        base_t = held.tile([P, seqs, blocks * tokens], BF16)
        offs_t = held.tile([P, entries // 16], U16)
        w_t = held.tile([P, feats], BF16)
        x_t = held.tile([P, entries], BF16)
        gain = held.tile([P, blocks], F32)
        shift = held.tile([P, blocks], F32)
        base_rows = base.rearrange("i (p a) t -> p i (a t)", p=P)
        for i in range(seqs):
            nc.sync.dma_start(base_t[:, i, :], base_rows[:, i, :])
        nc.sync.dma_start(offs_t[:], offs)
        nc.sync.dma_start(w_t[:], w)
        nc.sync.dma_start(x_t[:], x)
        nc.sync.dma_start(gain[:], s.rearrange("(p a) o -> p (a o)", p=P))
        nc.sync.dma_start(shift[:], b.rearrange("(p a) o -> p (a o)", p=P))

        early = held.tile([P, 1], F32)
        nc.vector.memset(early[:], 0.0)
        nc.scalar.activation(early[:], early[:], mybir.ActivationFunctionType.Identity)

        ident = held.tile([P, P], BF16)
        make_identity(nc, ident[:])

        windows = [psum.tile([P, tokens], F32, name=f"window{n}") for n in range(seqs * blocks)]
        for n, window in enumerate(windows):
            i, a = divmod(n, blocks)
            rows = base_t[:, i, a * tokens : (a + 1) * tokens]
            nc.tensor.matmul(window[:], ident[:], rows, start=True, stop=True)

        for n, window in enumerate(windows):
            i, a = divmod(n, blocks)
            places = offs_t[:, i * piece_cols : (i + 1) * piece_cols]
            nc.tensor.matmul(
                window[:].indirect(places),
                w_t[:, a::blocks],
                x_t[:, i * piece : (i + 1) * piece],
                start=True,
                stop=True,
            )

        out_rows = out.rearrange("i (p a) t -> p i (a t)", p=P)
        for i in range(seqs):
            for a in range(blocks):
                window = windows[i * blocks + a]
                result = held.tile([P, tokens], F32, name=f"result{i}_{a}")
                if a == 0:
                    nc.vector.tensor_scalar(
                        result[:],
                        window[:],
                        gain[:, a : a + 1],
                        shift[:, a : a + 1],
                        op0=mybir.AluOpType.mult,
                        op1=mybir.AluOpType.add,
                    )
                else:
                    nc.scalar.activation(
                        result[:],
                        window[:],
                        mybir.ActivationFunctionType.Identity,
                        bias=shift[:, a : a + 1],
                        scale=gain[:, a : a + 1],
                    )
                nc.sync.dma_start(out_rows[:, i, a * tokens : (a + 1) * tokens], result[:])
